import numpy as np
import ml_dtypes


def mxq(x, axis, fmt="e4m3"):
    dtype, down = {"e4m3": (ml_dtypes.float8_e4m3fn, 7), "e5m2": (ml_dtypes.float8_e5m2, 14)}[fmt]
    v = np.moveaxis(np.asarray(x, np.float32).astype(ml_dtypes.bfloat16).astype(np.float64), axis, -1)
    blocks = v.reshape(v.shape[:-1] + (-1, 32))
    amax = np.abs(blocks).max(-1, keepdims=True)
    byte = np.maximum(np.where(amax > 0, np.frexp(amax)[1] - 1 + 127, 0) - down, 1)
    scale = np.exp2(byte - 127.0)
    codes = (blocks / scale).astype(np.float32).astype(dtype).astype(np.float64)
    return np.moveaxis((codes * scale).reshape(v.shape), -1, axis)


WIDE = False


def mx_kscale(k):
    if not WIDE:
        return np.ones(k)
    levels = np.array([10, -10, 5, -5, 0])
    if k % 512:
        return np.exp2(np.random.permutation(np.resize(levels, k // 32))).repeat(32)
    a = np.empty((k // 512, 16))
    for p in range(k // 512):
        a[p, :8] = np.random.permutation(np.resize(levels, 8))
        for g in range(8):
            far = levels[np.abs(levels - a[p, g]) >= 10]
            a[p, g + 8] = far[np.random.randint(len(far))]
    return np.exp2(a.ravel()).repeat(32)


def f64(x):
    return np.asarray(x).astype(np.float64)


def striped(idx):
    return np.tile(idx.reshape(-1, 16).T, (8, 1)).astype(np.uint16)


def unstriped(offs):
    return offs[:16].T.reshape(-1).astype(np.int64)


def pack_weight(w):
    k, n = w.shape
    w = f64(np.asarray(w, np.float32).astype(ml_dtypes.bfloat16)).reshape(k // 32, 32, n)
    amax = np.abs(w).max(1)
    byte = np.clip(np.where(amax > 0, np.frexp(amax)[1] - 1 + 127 - 7, 1), 1, 254)
    scaled = (w * np.exp2(127.0 - byte)[:, None, :]).reshape(k, n).astype(np.float32)
    words = np.ascontiguousarray(scaled.reshape(k // 512, 128, 4, n).transpose(0, 1, 3, 2)).astype(ml_dtypes.float8_e4m3fn).view(np.uint8)
    return words, np.ascontiguousarray(byte.astype(np.uint8).reshape(k // 512, 16, n))


def unpack_weight(words, scales):
    g, p, n, _ = words.shape
    vals = np.ascontiguousarray(words).view(ml_dtypes.float8_e4m3fn).astype(np.float64) * np.repeat(np.exp2(scales.astype(np.float64) - 127.0), 8, axis=1)[..., None]
    return vals.transpose(0, 1, 3, 2).reshape(g * 512, n)


K, T, D, S, V, N = 1536, 512, 6, 1536, 256, 128


def setup_inputs():
    n = np.random.standard_normal
    s = mx_kscale(K)[:, None]
    words, scales = pack_weight(n((K, N)) / np.sqrt(K) / s)
    return {
        "xT": (n((K, T)) * s).astype(np.float32),
        "w_words": words,
        "w_scales": scales,
        "b": (0.3 * n((N, 1))).astype(np.float32),
        "gate": np.tile(np.random.uniform(0.2, 1.0, (D, 1, V)) / np.sqrt(D), (1, N, 1)).astype(np.float32),
        "pos1": striped(np.random.permutation(T)[:V]),
        "pos2": striped(np.random.permutation(T)[:V]),
        "pos3": striped(np.random.permutation(T)[:V]),
        "pos4": striped(np.random.permutation(T)[:V]),
        "pos5": striped(np.random.permutation(T)[:V]),
        "pos6": striped(np.random.permutation(T)[:V]),
    }


def reference(xT, w_words, w_scales, b, gate, pos1, pos2, pos3, pos4, pos5, pos6):
    w = unpack_weight(w_words, w_scales)
    y = w.T @ mxq(f64(xT), 0, "e4m3")
    y = y + f64(b)
    return sum(f64(gate[d]) * y[:, unstriped(p)] for d, p in enumerate((pos1, pos2, pos3, pos4, pos5, pos6)))

@@ -1,0 +1,144 @@
+from contextlib import ExitStack
+
+import concourse.mybir as mybir
+
+K, T, N, V, D = 1536, 512, 128, 256, 6
+FLOPS = 2 * K * T * N + 2 * D * N * V + T * N
+
+F32 = mybir.dt.float32
+BF16 = mybir.dt.bfloat16
+I32 = mybir.dt.int32
+U32 = mybir.dt.uint32
+U16 = mybir.dt.uint16
+U8 = mybir.dt.uint8
+FP8X4 = mybir.dt.float8_e4m3fn_x4
+IDENTITY = mybir.ActivationFunctionType.Identity
+MULT = mybir.AluOpType.mult
+
+P = 128
+PACK = 4
+K_PASS = P * PACK
+PASSES = K // K_PASS
+H = T // 2
+
+
+def tile_picked_agg_lin_bias_sub_l_kernel(tc, xT, w_words, w_scales, b, gate, pos1, pos2, pos3, pos4, pos5, pos6, out):
+    nc = tc.nc
+    with ExitStack() as ctx:
+        lists = ctx.enter_context(tc.tile_pool(name="lists", bufs=1))
+        keep = ctx.enter_context(tc.tile_pool(name="keep", bufs=1))
+        psum = ctx.enter_context(tc.psum_pool(name="psum", bufs=1))
+
+        offs = [lists.tile([P, V // 16], U16, name="offs%d" % d) for d in range(D)]
+        bias = keep.tile([P, 1], F32)
+        w_codes = keep.tile([P, PASSES, N], U32, align_bytes=64)
+        w_planes = keep.tile([P, N], U8, align_bytes=64)
+        warm = keep.tile([P, 2], F32)
+        gates = keep.tile([P, D, V], F32)
+        x_codes = keep.tile([P, PASSES, T], U32, align_bytes=64)
+        x_scales = keep.tile([P, PASSES, T], U8, align_bytes=64)
+        y = keep.tile([P, T], F32)
+
+        chunks = [(0, 0, T), (1, 0, T), (2, 0, H), (2, H, T)]
+        raws = [keep.tile([P, PACK, c1 - c0], F32, name="raw%d" % i) for i, (a, c0, c1) in enumerate(chunks)]
+        grouped = [keep.tile([P, c1 - c0, PACK], BF16, name="grouped%d" % i, align_bytes=64) for i, (a, c0, c1) in enumerate(chunks)]
+
+        def load(i):
+            a, c0, c1 = chunks[i]
+            nc.sync.dma_start(out=raws[i][:], in_=xT[a * K_PASS : (a + 1) * K_PASS, c0:c1].rearrange("(p j) t -> p j t", j=PACK))
+
+        nc.vector.memset(w_planes[:].bitcast(U32), 0)
+        nc.vector.memset(warm[:], 0.0)
+        nc.scalar.activation(warm[:, 0:1], warm[:, 1:2], IDENTITY)
+
+        nc.scalar.dma_start(out=bias[:], in_=b)
+        load(0)
+        nc.sync.dma_start(out=w_codes[:].rearrange("p a m -> p (a m)").bitcast(I32).rearrange("p (a m) -> p a m", a=PASSES), in_=w_words.rearrange("a p m r -> p a (m r)").bitcast(I32))
+        for q in range(4):
+            nc.gpsimd.dma_start(out=w_planes[32 * q : 32 * q + 4 * PASSES, :].bitcast(I32), in_=w_scales[:, 4 * q : 4 * q + 4, :].bitcast(I32))
+        poss = (pos1, pos2, pos3, pos4, pos5, pos6)
+        for d in range(4):
+            nc.sync.dma_start(offs[d][:], poss[d])
+        load(1)
+        load(2)
+        load(3)
+        nc.sync.dma_start(out=gates[:, 0:2, :], in_=gate[0:2].rearrange("d p v -> p d v"))
+        nc.sync.dma_start(offs[4][:], poss[4])
+        nc.sync.dma_start(out=gates[:, 2:6, :], in_=gate[2:6].rearrange("d p v -> p d v"))
+        nc.sync.dma_start(offs[5][:], poss[5])
+
+        def interleave(copy, i, t0, t1):
+            c0 = chunks[i][1]
+            copy(out=grouped[i][:, t0 - c0 : t1 - c0, :], in_=raws[i][:, :, t0 - c0 : t1 - c0].rearrange("p j t -> p t j"))
+
+        def quantize(i, t0, t1):
+            a, c0, c1 = chunks[i]
+            nc.vector.quantize_mx(
+                out=x_codes[:, a, t0:t1].bitcast(FP8X4),
+                scales=x_scales[:, a, t0:t1],
+                in_=grouped[i][:, t0 - c0 : t1 - c0, :].rearrange("p t j -> p (t j)"),
+            )
+
+        groups = [(0, H), (H, H + P), (H + P, T)]
+        sums = [psum.tile([P, t1 - t0], F32, name="sums%d" % g) for g, (t0, t1) in enumerate(groups)]
+
+        def multiply(a, g):
+            t0, t1 = groups[g]
+            nc.tensor.matmul_mx(
+                out=sums[g][:],
+                lhsT=w_codes[:, a, :].bitcast(FP8X4),
+                lhsT_scale=w_planes[4 * a :, :],
+                rhs=x_codes[:, a, t0:t1].bitcast(FP8X4),
+                rhs_scale=x_scales[:, a, t0:t1],
+                start=(a == 0),
+                stop=(a == PASSES - 1),
+            )
+
+        for a in range(2):
+            interleave(nc.scalar.copy, a, H, T)
+            interleave(nc.vector.tensor_copy, a, 0, H)
+            quantize(a, 0, H)
+            quantize(a, H, T)
+            for g in range(3):
+                multiply(a, g)
+        interleave(nc.scalar.copy, 2, P, H)
+        interleave(nc.vector.tensor_copy, 2, 0, P)
+        quantize(2, 0, H)
+        multiply(2, 0)
+        interleave(nc.scalar.copy, 3, T - 64, T)
+        interleave(nc.vector.tensor_copy, 3, H, H + P)
+        interleave(nc.vector.tensor_copy, 3, H + P, T - 64)
+        quantize(3, H, H + P)
+        quantize(3, H + P, T)
+        multiply(2, 1)
+        multiply(2, 2)
+        nc.scalar.activation(y[:, 0:H], sums[0][:], IDENTITY, bias=bias[:])
+        nc.scalar.activation(y[:, H : H + P], sums[1][:], IDENTITY, bias=bias[:])
+        nc.vector.tensor_scalar_add(y[:, H + P : T], sums[2][:], bias[:])
+
+        terms = [keep.tile([P, V], F32, name="term%d" % d) for d in range(D)]
+
+        def gather(d):
+            nc.vector.tensor_tensor(terms[d][:], y[:].indirect(offs[d][:]), gates[:, d, :], MULT)
+
+        s01 = keep.tile([P, V], F32)
+        s23 = keep.tile([P, V], F32)
+        s03 = keep.tile([P, V], F32)
+        s45 = keep.tile([P, V], F32)
+        result = keep.tile([P, V], F32)
+        gather(0)
+        gather(1)
+        gather(2)
+        nc.vector.tensor_add(s01[:], terms[0][:], terms[1][:])
+        gather(3)
+        gather(4)
+        nc.vector.tensor_add(s23[:], terms[2][:], terms[3][:])
+        gather(5)
+        nc.vector.tensor_add(s03[:], s01[:], s23[:])
+        for h in range(2):
+            c = slice(h * P, (h + 1) * P)
+            nc.vector.tensor_add(s45[:, c], terms[4][:, c], terms[5][:, c])
+        for h in range(2):
+            c = slice(h * P, (h + 1) * P)
+            nc.vector.tensor_add(result[:, c], s03[:, c], s45[:, c])
+        nc.sync.dma_start(out=out, in_=result[:])

@@ -32,14 +32,14 @@ def tile_picked_agg_lin_bias_sub_l_kernel(tc, xT, w_words, w_scales, b, gate, po
         offs = [lists.tile([P, V // 16], U16, name="offs%d" % d) for d in range(D)]
         bias = keep.tile([P, 1], F32)
         w_codes = keep.tile([P, PASSES, N], U32, align_bytes=64)
-        w_planes = keep.tile([P, N], U8, align_bytes=64)
+        w_planes = keep.tile([P, PASSES, N], U8, align_bytes=64)
         warm = keep.tile([P, 2], F32)
         gates = keep.tile([P, D, V], F32)
         x_codes = keep.tile([P, PASSES, T], U32, align_bytes=64)
         x_scales = keep.tile([P, PASSES, T], U8, align_bytes=64)
         y = keep.tile([P, T], F32)
 
-        chunks = [(0, 0, T), (1, 0, T), (2, 0, H), (2, H, T)]
+        chunks = [(0, 0, T), (1, 0, T), (2, 0, H + P), (2, H + P, T)]
         raws = [keep.tile([P, PACK, c1 - c0], F32, name="raw%d" % i) for i, (a, c0, c1) in enumerate(chunks)]
         grouped = [keep.tile([P, c1 - c0, PACK], BF16, name="grouped%d" % i, align_bytes=64) for i, (a, c0, c1) in enumerate(chunks)]
 
@@ -47,25 +47,23 @@ def tile_picked_agg_lin_bias_sub_l_kernel(tc, xT, w_words, w_scales, b, gate, po
             a, c0, c1 = chunks[i]
             nc.sync.dma_start(out=raws[i][:], in_=xT[a * K_PASS : (a + 1) * K_PASS, c0:c1].rearrange("(p j) t -> p j t", j=PACK))
 
-        nc.vector.memset(w_planes[:].bitcast(U32), 0)
-        nc.vector.memset(warm[:], 0.0)
-        nc.scalar.activation(warm[:, 0:1], warm[:, 1:2], IDENTITY)
-
+        for q in range(4):
+            nc.scalar.dma_start(out=w_planes[32 * q : 32 * q + 4, :, :].bitcast(I32), in_=w_scales[:, 4 * q : 4 * q + 4, :].rearrange("a q m -> q a m").bitcast(I32))
         nc.scalar.dma_start(out=bias[:], in_=b)
         load(0)
         nc.sync.dma_start(out=w_codes[:].rearrange("p a m -> p (a m)").bitcast(I32).rearrange("p (a m) -> p a m", a=PASSES), in_=w_words.rearrange("a p m r -> p a (m r)").bitcast(I32))
-        for q in range(4):
-            nc.gpsimd.dma_start(out=w_planes[32 * q : 32 * q + 4 * PASSES, :].bitcast(I32), in_=w_scales[:, 4 * q : 4 * q + 4, :].bitcast(I32))
-        poss = (pos1, pos2, pos3, pos4, pos5, pos6)
-        for d in range(4):
-            nc.sync.dma_start(offs[d][:], poss[d])
         load(1)
         load(2)
         load(3)
+        poss = (pos1, pos2, pos3, pos4, pos5, pos6)
+        nc.sync.dma_start(offs[0][:], poss[0])
         nc.sync.dma_start(out=gates[:, 0:2, :], in_=gate[0:2].rearrange("d p v -> p d v"))
-        nc.sync.dma_start(offs[4][:], poss[4])
+        nc.sync.dma_start(offs[1][:], poss[1])
         nc.sync.dma_start(out=gates[:, 2:6, :], in_=gate[2:6].rearrange("d p v -> p d v"))
-        nc.sync.dma_start(offs[5][:], poss[5])
+        for d in range(2, 6):
+            nc.sync.dma_start(offs[d][:], poss[d])
+        nc.vector.memset(warm[:], 0.0)
+        nc.scalar.activation(warm[:, 0:1], warm[:, 1:2], IDENTITY)
 
         def interleave(copy, i, t0, t1):
             c0 = chunks[i][1]
@@ -87,7 +85,7 @@ def tile_picked_agg_lin_bias_sub_l_kernel(tc, xT, w_words, w_scales, b, gate, po
             nc.tensor.matmul_mx(
                 out=sums[g][:],
                 lhsT=w_codes[:, a, :].bitcast(FP8X4),
-                lhsT_scale=w_planes[4 * a :, :],
+                lhsT_scale=w_planes[:, a, :],
                 rhs=x_codes[:, a, t0:t1].bitcast(FP8X4),
                 rhs_scale=x_scales[:, a, t0:t1],
                 start=(a == 0),
@@ -101,44 +99,33 @@ def tile_picked_agg_lin_bias_sub_l_kernel(tc, xT, w_words, w_scales, b, gate, po
             quantize(a, H, T)
             for g in range(3):
                 multiply(a, g)
-        interleave(nc.scalar.copy, 2, P, H)
-        interleave(nc.vector.tensor_copy, 2, 0, P)
+        interleave(nc.scalar.copy, 2, H, H + P)
+        interleave(nc.vector.tensor_copy, 2, 0, H)
         quantize(2, 0, H)
+        quantize(2, H, H + P)
         multiply(2, 0)
-        interleave(nc.scalar.copy, 3, T - 64, T)
-        interleave(nc.vector.tensor_copy, 3, H, H + P)
-        interleave(nc.vector.tensor_copy, 3, H + P, T - 64)
-        quantize(3, H, H + P)
-        quantize(3, H + P, T)
         multiply(2, 1)
+        interleave(nc.scalar.copy, 3, T - 48, T)
+        interleave(nc.vector.tensor_copy, 3, H + P, T - 48)
+        quantize(3, H + P, T)
         multiply(2, 2)
         nc.scalar.activation(y[:, 0:H], sums[0][:], IDENTITY, bias=bias[:])
         nc.scalar.activation(y[:, H : H + P], sums[1][:], IDENTITY, bias=bias[:])
         nc.vector.tensor_scalar_add(y[:, H + P : T], sums[2][:], bias[:])
 
-        terms = [keep.tile([P, V], F32, name="term%d" % d) for d in range(D)]
-
-        def gather(d):
-            nc.vector.tensor_tensor(terms[d][:], y[:].indirect(offs[d][:]), gates[:, d, :], MULT)
-
-        s01 = keep.tile([P, V], F32)
-        s23 = keep.tile([P, V], F32)
-        s03 = keep.tile([P, V], F32)
-        s45 = keep.tile([P, V], F32)
+        terms = keep.tile([P, D, V], F32)
+        pairs = keep.tile([P, 2, V], F32)
+        even = keep.tile([P, V], F32)
+        odd = keep.tile([P, V], F32)
         result = keep.tile([P, V], F32)
-        gather(0)
-        gather(1)
-        gather(2)
-        nc.vector.tensor_add(s01[:], terms[0][:], terms[1][:])
-        gather(3)
-        gather(4)
-        nc.vector.tensor_add(s23[:], terms[2][:], terms[3][:])
-        gather(5)
-        nc.vector.tensor_add(s03[:], s01[:], s23[:])
-        for h in range(2):
-            c = slice(h * P, (h + 1) * P)
-            nc.vector.tensor_add(s45[:, c], terms[4][:, c], terms[5][:, c])
-        for h in range(2):
-            c = slice(h * P, (h + 1) * P)
-            nc.vector.tensor_add(result[:, c], s03[:, c], s45[:, c])
+        for d in range(D):
+            nc.vector.tensor_tensor(terms[:, d, :], y[:].indirect(offs[d][:]), gates[:, d, :], MULT)
+            if d == 4:
+                nc.vector.tensor_add(pairs[:], terms[:, 0:2, :], terms[:, 2:4, :])
+        nc.vector.tensor_add(even[:], pairs[:, 0, :], terms[:, 4, :])
+        halves = (slice(0, V // 2), slice(V // 2, V))
+        for c in halves:
+            nc.vector.tensor_add(odd[:, c], pairs[:, 1, c], terms[:, 5, c])
+        for c in halves:
+            nc.vector.tensor_add(result[:, c], even[:, c], odd[:, c])
         nc.sync.dma_start(out=out, in_=result[:])

from contextlib import ExitStack

import concourse.mybir as mybir

K, T, N, V, D = 1536, 512, 128, 256, 6
FLOPS = 2 * K * T * N + 2 * D * N * V + T * N

F32 = mybir.dt.float32
BF16 = mybir.dt.bfloat16
I32 = mybir.dt.int32
U32 = mybir.dt.uint32
U16 = mybir.dt.uint16
U8 = mybir.dt.uint8
FP8X4 = mybir.dt.float8_e4m3fn_x4
IDENTITY = mybir.ActivationFunctionType.Identity
MULT = mybir.AluOpType.mult

P = 128
PACK = 4
K_PASS = P * PACK
PASSES = K // K_PASS
H = T // 2


def tile_picked_agg_lin_bias_sub_l_kernel(tc, xT, w_words, w_scales, b, gate, pos1, pos2, pos3, pos4, pos5, pos6, out):
    nc = tc.nc
    with ExitStack() as ctx:
        lists = ctx.enter_context(tc.tile_pool(name="lists", bufs=1))
        keep = ctx.enter_context(tc.tile_pool(name="keep", bufs=1))
        psum = ctx.enter_context(tc.psum_pool(name="psum", bufs=1))

        offs = [lists.tile([P, V // 16], U16, name="offs%d" % d) for d in range(D)]
        bias = keep.tile([P, 1], F32)
        w_codes = keep.tile([P, PASSES, N], U32, align_bytes=64)
        w_planes = keep.tile([P, PASSES, N], U8, align_bytes=64)
        warm = keep.tile([P, 2], F32)
        gates = keep.tile([P, D, V], F32)
        x_codes = keep.tile([P, PASSES, T], U32, align_bytes=64)
        x_scales = keep.tile([P, PASSES, T], U8, align_bytes=64)
        y = keep.tile([P, T], F32)

        chunks = [(0, 0, T), (1, 0, T), (2, 0, H + P), (2, H + P, T)]
        raws = [keep.tile([P, PACK, c1 - c0], F32, name="raw%d" % i) for i, (a, c0, c1) in enumerate(chunks)]
        grouped = [keep.tile([P, c1 - c0, PACK], BF16, name="grouped%d" % i, align_bytes=64) for i, (a, c0, c1) in enumerate(chunks)]

        def load(i):
            a, c0, c1 = chunks[i]
            nc.sync.dma_start(out=raws[i][:], in_=xT[a * K_PASS : (a + 1) * K_PASS, c0:c1].rearrange("(p j) t -> p j t", j=PACK))

        for q in range(4):
            nc.scalar.dma_start(out=w_planes[32 * q : 32 * q + 4, :, :].bitcast(I32), in_=w_scales[:, 4 * q : 4 * q + 4, :].rearrange("a q m -> q a m").bitcast(I32))
        nc.scalar.dma_start(out=bias[:], in_=b)
        load(0)
        nc.sync.dma_start(out=w_codes[:].rearrange("p a m -> p (a m)").bitcast(I32).rearrange("p (a m) -> p a m", a=PASSES), in_=w_words.rearrange("a p m r -> p a (m r)").bitcast(I32))
        load(1)
        load(2)
        load(3)
        poss = (pos1, pos2, pos3, pos4, pos5, pos6)
        nc.sync.dma_start(offs[0][:], poss[0])
        nc.sync.dma_start(out=gates[:, 0:2, :], in_=gate[0:2].rearrange("d p v -> p d v"))
        nc.sync.dma_start(offs[1][:], poss[1])
        nc.sync.dma_start(out=gates[:, 2:6, :], in_=gate[2:6].rearrange("d p v -> p d v"))
        for d in range(2, 6):
            nc.sync.dma_start(offs[d][:], poss[d])
        nc.vector.memset(warm[:], 0.0)
        nc.scalar.activation(warm[:, 0:1], warm[:, 1:2], IDENTITY)

        def interleave(copy, i, t0, t1):
            c0 = chunks[i][1]
            copy(out=grouped[i][:, t0 - c0 : t1 - c0, :], in_=raws[i][:, :, t0 - c0 : t1 - c0].rearrange("p j t -> p t j"))

        def quantize(i, t0, t1):
            a, c0, c1 = chunks[i]
            nc.vector.quantize_mx(
                out=x_codes[:, a, t0:t1].bitcast(FP8X4),
                scales=x_scales[:, a, t0:t1],
                in_=grouped[i][:, t0 - c0 : t1 - c0, :].rearrange("p t j -> p (t j)"),
            )

        groups = [(0, H), (H, H + P), (H + P, T)]
        sums = [psum.tile([P, t1 - t0], F32, name="sums%d" % g) for g, (t0, t1) in enumerate(groups)]

        def multiply(a, g):
            t0, t1 = groups[g]
            nc.tensor.matmul_mx(
                out=sums[g][:],
                lhsT=w_codes[:, a, :].bitcast(FP8X4),
                lhsT_scale=w_planes[:, a, :],
                rhs=x_codes[:, a, t0:t1].bitcast(FP8X4),
                rhs_scale=x_scales[:, a, t0:t1],
                start=(a == 0),
                stop=(a == PASSES - 1),
            )

        for a in range(2):
            interleave(nc.scalar.copy, a, H, T)
            interleave(nc.vector.tensor_copy, a, 0, H)
            quantize(a, 0, H)
            quantize(a, H, T)
            for g in range(3):
                multiply(a, g)
        interleave(nc.scalar.copy, 2, H, H + P)
        interleave(nc.vector.tensor_copy, 2, 0, H)
        quantize(2, 0, H)
        quantize(2, H, H + P)
        multiply(2, 0)
        multiply(2, 1)
        interleave(nc.scalar.copy, 3, T - 48, T)
        interleave(nc.vector.tensor_copy, 3, H + P, T - 48)
        quantize(3, H + P, T)
        multiply(2, 2)
        nc.scalar.activation(y[:, 0:H], sums[0][:], IDENTITY, bias=bias[:])
        nc.scalar.activation(y[:, H : H + P], sums[1][:], IDENTITY, bias=bias[:])
        nc.vector.tensor_scalar_add(y[:, H + P : T], sums[2][:], bias[:])

        terms = keep.tile([P, D, V], F32)
        pairs = keep.tile([P, 2, V], F32)
        even = keep.tile([P, V], F32)
        odd = keep.tile([P, V], F32)
        result = keep.tile([P, V], F32)
        for d in range(D):
            nc.vector.tensor_tensor(terms[:, d, :], y[:].indirect(offs[d][:]), gates[:, d, :], MULT)
            if d == 4:
                nc.vector.tensor_add(pairs[:], terms[:, 0:2, :], terms[:, 2:4, :])
        nc.vector.tensor_add(even[:], pairs[:, 0, :], terms[:, 4, :])
        halves = (slice(0, V // 2), slice(V // 2, V))
        for c in halves:
            nc.vector.tensor_add(odd[:, c], pairs[:, 1, c], terms[:, 5, c])
        for c in halves:
            nc.vector.tensor_add(result[:, c], even[:, c], odd[:, c])
        nc.sync.dma_start(out=out, in_=result[:])
